import numpy as np
import ml_dtypes


def mxq(x, axis, fmt="e4m3"):
    dtype, down = {"e4m3": (ml_dtypes.float8_e4m3fn, 7), "e5m2": (ml_dtypes.float8_e5m2, 14)}[fmt]
    v = np.moveaxis(np.asarray(x, np.float32).astype(ml_dtypes.bfloat16).astype(np.float64), axis, -1)
    blocks = v.reshape(v.shape[:-1] + (-1, 32))
    amax = np.abs(blocks).max(-1, keepdims=True)
    byte = np.maximum(np.where(amax > 0, np.frexp(amax)[1] - 1 + 127, 0) - down, 1)
    scale = np.exp2(byte - 127.0)
    codes = (blocks / scale).astype(np.float32).astype(dtype).astype(np.float64)
    return np.moveaxis((codes * scale).reshape(v.shape), -1, axis)


WIDE = False


def mx_kscale(k):
    if not WIDE:
        return np.ones(k)
    levels = np.array([10, -10, 5, -5, 0])
    if k % 512:
        return np.exp2(np.random.permutation(np.resize(levels, k // 32))).repeat(32)
    a = np.empty((k // 512, 16))
    for p in range(k // 512):
        a[p, :8] = np.random.permutation(np.resize(levels, 8))
        for g in range(8):
            far = levels[np.abs(levels - a[p, g]) >= 10]
            a[p, g + 8] = far[np.random.randint(len(far))]
    return np.exp2(a.ravel()).repeat(32)


def f64(x):
    return np.asarray(x).astype(np.float64)


def striped(idx):
    return np.tile(np.asarray(idx).reshape(-1, 16).T, (8, 1)).astype(np.uint16)


def unstriped(offs):
    return offs[:16].T.reshape(-1).astype(np.int64)


E2M1 = np.array([0.0, 0.5, 1.0, 1.5, 2.0, 3.0, 4.0, 6.0, -0.0, -0.5, -1.0, -1.5, -2.0, -3.0, -4.0, -6.0])


def pack_weight(w, fmt):
    k, n = w.shape
    w = f64(np.asarray(w, np.float32).astype(ml_dtypes.bfloat16)).reshape(k // 32, 32, n)
    amax = np.abs(w).max(1)
    if fmt == "e4m3":
        byte = np.frexp(amax)[1] - 1 + 127 - 7
    else:
        mant, ex = np.frexp(amax / 6.0)
        byte = np.where(mant > 0.5, ex, ex - 1) + 127
    byte = np.clip(np.where(amax > 0, byte, 1), 1, 254)
    scaled = (w * np.exp2(127.0 - byte)[:, None, :]).reshape(k, n).astype(np.float32)
    by_word = np.ascontiguousarray(scaled.reshape(k // 512, 128, 4, n).transpose(0, 1, 3, 2))
    if fmt == "e4m3":
        words = by_word.astype(ml_dtypes.float8_e4m3fn).view(np.uint8)
    else:
        c = by_word.astype(ml_dtypes.float4_e2m1fn).view(np.uint8) & 0xF
        words = (c[..., 0::2] | (c[..., 1::2] << 4)).reshape(k // 512, 128, 2 * n)
    return np.ascontiguousarray(words), np.ascontiguousarray(byte.astype(np.uint8).reshape(k // 512, 16, n))


def unpack_weight(words, scales, fmt):
    g, _, n = scales.shape
    words = np.ascontiguousarray(words).reshape(g, 128, n, -1)
    if fmt == "e4m3":
        vals = words.view(ml_dtypes.float8_e4m3fn).astype(np.float64)
    else:
        nib = np.empty((g, 128, n, 4), np.uint8)
        nib[..., 0::2] = words & 0xF
        nib[..., 1::2] = words >> 4
        vals = E2M1[nib]
    vals = vals * np.repeat(np.exp2(scales.astype(np.float64) - 127.0), 8, axis=1)[..., None]
    return vals.transpose(0, 1, 3, 2).reshape(g * 512, n)


D, T, I, J, U, X, Z, E = 512, 2048, 512, 512, 1024, 1024, 1024, 512


def setup_inputs():
    n = np.random.standard_normal
    idx = np.random.permutation(T)[:I]
    idx2 = np.random.permutation(U)[:J]
    idx3 = np.random.permutation(X)[:I]
    idx4 = np.random.permutation(Z)[:J]
    fd = mx_kscale(D)
    fi = mx_kscale(I)
    ti = np.ones(T)
    ti[idx] = fi
    keysp = pack_weight(n((D, T)) / fd[:, None], "e4m3")
    morep = pack_weight(n((D, X)) / fd[:, None], "e4m3")
    return {
        "keys_words": keysp[0],
        "keys_scales": keysp[1],
        "notes": (n((D, U)) * 1.0 / np.sqrt(D) * fd[:, None]).astype(np.float32),
        "more_words": morep[0],
        "more_scales": morep[1],
        "users2": (n((D, Z)) * 1.0 / np.sqrt(D) * fd[:, None]).astype(np.float32),
        "rowf": (np.random.uniform(0.02, 0.08, (I, 1)) * fi[:, None]).astype(np.float32),
        "vals": (n((E, T)) / ti).astype(np.float32),
        "offs": striped(idx),
        "offs2": striped(idx2),
        "offs3": striped(idx3),
        "offs4": striped(idx4),
    }


def reference(keys_words, keys_scales, notes, more_words, more_scales, users2, rowf, vals, offs, offs2, offs3, offs4):
    idx = unstriped(offs)
    idx2 = unstriped(offs2)
    idx3 = unstriped(offs3)
    idx4 = unstriped(offs4)
    keysu = unpack_weight(keys_words, keys_scales, "e4m3")
    moreu = unpack_weight(more_words, more_scales, "e4m3")
    keysidxg = keysu[:, idx]
    notesidx2q = mxq(f64(notes)[:, idx2], 0, "e4m3")
    moreidx3g = moreu[:, idx3]
    users2idx4q = mxq(f64(users2)[:, idx4], 0, "e4m3")
    g9 = keysidxg.T @ notesidx2q + moreidx3g.T @ users2idx4q
    g0 = np.maximum(g9, 0.0)
    gr1 = g0 * f64(rowf)
    vt1 = f64(vals)[:, idx].T
    vt1q = mxq(vt1, 0, "e4m3")
    gr1q = mxq(gr1, 0, "e4m3")
    o = vt1q.T @ gr1q
    return o

@@ -1,0 +1,251 @@
+from contextlib import ExitStack
+
+import concourse.mybir as mybir
+from concourse.masks import make_identity
+
+D, T, I, J, U, X, Z, E = 512, 2048, 512, 512, 1024, 1024, 1024, 512
+FLOPS = 2 * (2 * D * I * J + I * E * J)
+
+F32 = mybir.dt.float32
+BF16 = mybir.dt.bfloat16
+I32 = mybir.dt.int32
+U32 = mybir.dt.uint32
+U16 = mybir.dt.uint16
+U8 = mybir.dt.uint8
+FP8X4 = mybir.dt.float8_e4m3fn_x4
+COPY = mybir.ActivationFunctionType.Copy
+ALU = mybir.AluOpType
+
+P = 128
+PACK = 4
+LIST_COLS = I // 16
+MORE_ROW = 4
+WINDOW_BYTES = 4 * T
+KEYS_AT = 4 * WINDOW_BYTES
+NOTES_GROUPED_AT = KEYS_AT + 4 * T
+VALS_GROUPED_AT = NOTES_GROUPED_AT + 2 * PACK * J
+BLOCK_BYTES = 2 * I
+PICKED_AT = (KEYS_AT, KEYS_AT + BLOCK_BYTES, WINDOW_BYTES, VALS_GROUPED_AT + BLOCK_BYTES // 2)
+GROUPED_AT = (WINDOW_BYTES, VALS_GROUPED_AT, VALS_GROUPED_AT + BLOCK_BYTES, VALS_GROUPED_AT + 2 * BLOCK_BYTES)
+ACC_BANK = (("table0",), ("table1",), ("table2",), ("table3", "bank0"))
+
+
+def tile_attend_tab_twosum_exchange_kernel(
+    tc, keys_words, keys_scales, notes, more_words, more_scales, users2, rowf, vals, offs, offs2, offs3, offs4, out
+):
+    nc = tc.nc
+    with ExitStack() as ctx:
+        lists = ctx.enter_context(tc.tile_pool(name="lists", bufs=1))
+        keep = ctx.enter_context(tc.tile_pool(name="keep", bufs=1))
+        windows = ctx.enter_context(tc.tile_pool(name="windows", bufs=1))
+        psum = ctx.enter_context(tc.psum_pool(name="psum", bufs=1))
+
+        def load_list(name, src):
+            tile = lists.tile([P, LIST_COLS], U16, name=name)
+            nc.sync.dma_start(tile[:], src)
+            return tile
+
+        def load_rows(name, src):
+            tile = keep.tile([P, src.shape[1]], F32, name=name, tag=name, align_bytes=64)
+            nc.sync.dma_start(tile[:], src)
+            return tile
+
+        def load_words(name, src):
+            tile = keep.tile([P, src.shape[2]], U32, name=name)
+            nc.sync.dma_start(tile[:].bitcast(I32), src[0].rearrange("p n t -> p (n t)").bitcast(I32))
+            return tile
+
+        def zeroed_scale_tile(name, src):
+            tile = keep.tile([P, src.shape[2]], U8, name=name)
+            nc.gpsimd.memset(tile[:].bitcast(I32), 0)
+            return tile
+
+        def load_scale_rows(tile, src, row, c):
+            nc.sync.dma_start(tile[row + c : P : 32, :].bitcast(I32), src[0, c:16:4, :].bitcast(I32))
+
+        def gather_scalar(dst, window, offsets):
+            nc.scalar.activation(dst, window[:].indirect(offsets), COPY)
+
+        def gather_vector(dst, window, offsets):
+            nc.vector.tensor_copy(dst, window[:].indirect(offsets))
+
+        def gather_dealt(name, dtype, window, offsets):
+            tile = keep.tile([P, I], dtype, name=name, align_bytes=64)
+            nc.vector.tensor_copy(tile[:].rearrange("q (r s) -> q s r", r=PACK), window[:].indirect(offsets[:]))
+            return tile
+
+        def mx_tiles(name, width, codes_tag=None):
+            codes = keep.tile([P, width], U32, name=name + "_codes", tag=codes_tag or name + "_codes", align_bytes=64)
+            scales = keep.tile([P, width], U8, name=name + "_scales", align_bytes=64)
+            return codes, scales
+
+        def quantize(codes, scales, grouped):
+            nc.vector.quantize_mx(out=codes.bitcast(FP8X4), scales=scales, in_=grouped)
+
+        def interleave(copy, grouped, planes):
+            copy(grouped.rearrange("p (c i) t -> p c t i", i=4), planes.rearrange("p t (c i) -> p c t i", i=4))
+
+        more_scale_pool = zeroed_scale_tile("more_scale_pool", more_scales)
+        keys_scale_pool = zeroed_scale_tile("keys_scale_pool", keys_scales)
+        notes_rows = notes.rearrange("(p t) u -> t p u", t=PACK)
+        users_rows = users2.rearrange("(p t) z -> t p z", t=PACK)
+        more_pool = load_words("more_pool", more_words)
+        list_more = load_list("list_more", offs3)
+        users_pool = [load_rows("users0", users_rows[0])]
+        list_users = load_list("list_users", offs4)
+        load_scale_rows(more_scale_pool, more_scales, MORE_ROW, 0)
+        load_scale_rows(more_scale_pool, more_scales, MORE_ROW, 1)
+        users_pool.append(load_rows("users1", users_rows[1]))
+        load_scale_rows(more_scale_pool, more_scales, MORE_ROW, 2)
+        load_scale_rows(more_scale_pool, more_scales, MORE_ROW, 3)
+        users_pool.append(load_rows("users2", users_rows[2]))
+        list_tokens = load_list("list_tokens", offs)
+        load_scale_rows(keys_scale_pool, keys_scales, 0, 0)
+        users_pool.append(load_rows("users3", users_rows[3]))
+        load_scale_rows(keys_scale_pool, keys_scales, 0, 1)
+        load_scale_rows(keys_scale_pool, keys_scales, 0, 2)
+        load_scale_rows(keys_scale_pool, keys_scales, 0, 3)
+        notes_pool = [load_rows("notes0", notes_rows[0])]
+        list_notes = load_list("list_notes", offs2)
+        notes_pool.append(load_rows("notes1", notes_rows[1]))
+        factor = keep.tile([P, PACK], F32, name="factor")
+        nc.sync.dma_start(factor[:], rowf.rearrange("(p r) o -> p (r o)", r=PACK))
+        notes_pool.append(load_rows("notes2", notes_rows[2]))
+        notes_pool.append(load_rows("notes3", notes_rows[3]))
+        keys_pool = windows.tile([P, T], U32, name="keys_pool", offset=KEYS_AT)
+        nc.sync.dma_start(keys_pool[:].bitcast(I32), keys_words[0].rearrange("p n t -> p (n t)").bitcast(I32))
+        vals_pool = []
+        for b in range(E // P):
+            window = windows.tile([P, T], F32, name="vals%d" % b, offset=b * WINDOW_BYTES)
+            nc.sync.dma_start(window[:], vals[P * b : P * (b + 1), :])
+            vals_pool.append(window)
+
+        identity = keep.tile([P, P], F32, name="identity")
+        make_identity(nc, identity[:])
+
+        more_cd = gather_dealt("more_cd", U32, more_pool, list_more)
+        users_planes = keep.tile([P, PACK, J], BF16, name="users_planes")
+        for t in range(PACK):
+            gather = gather_vector if t == 1 else gather_scalar
+            gather(users_planes[:, t, :], users_pool[t], list_users[:])
+        more_sc = gather_dealt("more_sc", U8, more_scale_pool, list_more)
+        keys_sc = gather_dealt("keys_sc", U8, keys_scale_pool, list_tokens)
+        users_grouped = keep.tile([P, J, PACK], BF16, name="users_grouped", align_bytes=64)
+        interleave(nc.vector.tensor_copy, users_grouped[:], users_planes[:])
+        users_codes, users_scales = mx_tiles("users", J)
+        quantize(users_codes[:], users_scales[:], users_grouped[:].rearrange("p j t -> p (j t)"))
+        notes_planes = keep.tile([P, PACK, J], BF16, name="notes_planes")
+        gather_vector(notes_planes[:, 0, :], notes_pool[0], list_notes[:])
+        gather_scalar(notes_planes[:, 1, :], notes_pool[1], list_notes[:])
+        gather_scalar(notes_planes[:, 2, :], notes_pool[2], list_notes[:])
+        notes_grouped = windows.tile([P, J, PACK], BF16, name="notes_grouped", align_bytes=64, offset=NOTES_GROUPED_AT)
+        notes_codes, notes_scales = mx_tiles("notes", J)
+        for h, (gather, copy) in enumerate(((gather_vector, nc.vector.tensor_copy), (gather_scalar, nc.scalar.copy))):
+            cols = slice(h * J // 2, (h + 1) * J // 2)
+            entries = slice(h * LIST_COLS // 2, (h + 1) * LIST_COLS // 2)
+            gather(notes_planes[:, PACK - 1, cols], notes_pool[PACK - 1], list_notes[:, entries])
+            interleave(copy, notes_grouped[:, cols, :], notes_planes[:, :, cols])
+            quantize(notes_codes[:, cols], notes_scales[:, cols], notes_grouped[:, cols, :].rearrange("p j t -> p (j t)"))
+        keys_cd = windows.tile([P, I], U32, name="keys_cd", align_bytes=64, offset=NOTES_GROUPED_AT)
+        nc.vector.tensor_copy(keys_cd[:].rearrange("q (r s) -> q s r", r=PACK), keys_pool[:].indirect(list_tokens[:]))
+
+        table = [psum.tile([P, PACK, P], F32, name="table%d" % c, tag="table%d" % c) for c in range(J // P)]
+        terms = (
+            (more_cd, more_sc, MORE_ROW, users_codes, users_scales),
+            (keys_cd, keys_sc, 0, notes_codes, notes_scales),
+        )
+        for term, (lhs_codes, lhs_scales, row, rhs_codes, rhs_scales) in enumerate(terms):
+            for c in range(J // P):
+                cols = slice(P * c, P * (c + 1))
+                for r in range(PACK):
+                    rows = slice(P * r, P * (r + 1))
+                    nc.tensor.matmul_mx(
+                        out=table[c][:, r, :],
+                        lhsT=lhs_codes[:, rows].bitcast(FP8X4),
+                        lhsT_scale=lhs_scales[row:P, rows],
+                        rhs=rhs_codes[:, cols].bitcast(FP8X4),
+                        rhs_scale=rhs_scales[:, cols],
+                        start=(term == 0 and r == 0),
+                        stop=(term == len(terms) - 1 and r == PACK - 1),
+                    )
+
+        weighted = keep.tile([P, J, PACK], BF16, name="weighted", tag="weighted", align_bytes=64)
+        weighted_codes, weighted_scales = mx_tiles("weighted", J)
+        for c in range(J // P):
+            nc.vector.scalar_tensor_tensor(
+                out=weighted[:, P * c : P * (c + 1), :],
+                in0=table[c][:].rearrange("p r j -> p j r"),
+                scalar=0.0,
+                in1=factor[:].unsqueeze(1).to_broadcast([P, P, PACK]),
+                op0=ALU.max,
+                op1=ALU.mult,
+            )
+        for h in range(2):
+            cols = slice(h * J // 2, (h + 1) * J // 2)
+            quantize(weighted_codes[:, cols], weighted_scales[:, cols], weighted[:, cols, :].rearrange("p j r -> p (j r)"))
+
+        last = E // P - 1
+
+        def pick(b):
+            picked = windows.tile([P, I], BF16, name="picked%d" % b, offset=PICKED_AT[b])
+            if b < last - 1:
+                gather_scalar(picked[:], vals_pool[b], list_tokens[:])
+            else:
+                gather_scalar(picked[:, : I // 2], vals_pool[b], list_tokens[:, : LIST_COLS // 2])
+                gather_vector(picked[:, I // 2 :], vals_pool[b], list_tokens[:, LIST_COLS // 2 :])
+            return picked
+
+        def turn(b, picked):
+            turned = psum.tile([P, 2, P], F32, name="turned%d" % b, tag="bank%d" % b)
+            words = picked[:].bitcast(F32)
+            for u in range(2):
+                nc.tensor.transpose(turned[:, u, :], words[:, u : I // 2 : 2], identity[:])
+            vals_grouped = windows.tile([P, P, PACK], BF16, name="vals_grouped%d" % b, align_bytes=64, offset=GROUPED_AT[b])
+            nc.scalar.copy(vals_grouped[:].bitcast(F32), turned[:].rearrange("p u e -> p e u"))
+            return vals_grouped
+
+        def quantize_values(b, vals_grouped):
+            if b == 1:
+                vals_codes = windows.tile([P, P], U32, name="vals1_codes", align_bytes=64, offset=2 * WINDOW_BYTES + 4 * J)
+                vals_scales = keep.tile([P, P], U8, name="vals1_scales", align_bytes=64)
+            else:
+                vals_codes, vals_scales = mx_tiles("vals%d" % b, P, "weighted" if b == 0 else None)
+            quantize(vals_codes[:], vals_scales[:], vals_grouped[:].rearrange("p e r -> p (e r)"))
+            return vals_codes, vals_scales
+
+        def multiply(b, operand, result):
+            vals_codes, vals_scales = operand
+            parts = 1 if b < last else 2
+            for h in range(parts):
+                cols = slice(h * J // parts, (h + 1) * J // parts)
+                acc = psum.tile([P, J // parts], F32, name="acc%d_%d" % (b, h), tag=ACC_BANK[b][h])
+                nc.tensor.matmul_mx(
+                    out=acc[:],
+                    lhsT=vals_codes[:].bitcast(FP8X4),
+                    lhsT_scale=vals_scales[:],
+                    rhs=weighted_codes[:, cols].bitcast(FP8X4),
+                    rhs_scale=weighted_scales[:, cols],
+                    start=True,
+                    stop=True,
+                )
+                if b >= last - 1 and h == 0:
+                    nc.scalar.copy(result[:, cols], acc[:])
+                else:
+                    nc.vector.tensor_copy(result[:, cols], acc[:])
+                queue = nc.scalar if b == last and h == 0 else nc.sync
+                queue.dma_start(out[P * b : P * (b + 1), cols], result[:, cols])
+
+        picked_first = [pick(b) for b in range(2)]
+        grouped_first = [turn(b, picked_first[b]) for b in range(2)]
+        operand0 = quantize_values(0, grouped_first[0])
+        picked2 = pick(2)
+        result_first = windows.tile([P, J], F32, name="result_first", offset=2 * WINDOW_BYTES)
+        multiply(0, operand0, result_first)
+        operand1 = quantize_values(1, grouped_first[1])
+        operand2 = quantize_values(2, turn(2, picked2))
+        picked_last = pick(last)
+        result_middle = windows.tile([P, 2 * J], F32, name="result_middle", offset=last * WINDOW_BYTES)
+        multiply(1, operand1, result_middle[:, :J])
+        multiply(2, operand2, result_middle[:, J:])
+        result_last = keep.tile([P, J], F32, name="result_last")
+        multiply(last, quantize_values(last, turn(last, picked_last)), result_last)

@@ -120,8 +120,10 @@ def tile_attend_tab_twosum_exchange_kernel(
             nc.sync.dma_start(window[:], vals[P * b : P * (b + 1), :])
             vals_pool.append(window)
 
+        identity_bf16 = keep.tile([P, P], BF16, name="identity_bf16")
+        make_identity(nc, identity_bf16[:])
         identity = keep.tile([P, P], F32, name="identity")
-        make_identity(nc, identity[:])
+        nc.scalar.activation(identity[:], identity_bf16[:], COPY)
 
         more_cd = gather_dealt("more_cd", U32, more_pool, list_more)
         users_planes = keep.tile([P, PACK, J], BF16, name="users_planes")
@@ -135,9 +137,9 @@ def tile_attend_tab_twosum_exchange_kernel(
         users_codes, users_scales = mx_tiles("users", J)
         quantize(users_codes[:], users_scales[:], users_grouped[:].rearrange("p j t -> p (j t)"))
         notes_planes = keep.tile([P, PACK, J], BF16, name="notes_planes")
-        gather_vector(notes_planes[:, 0, :], notes_pool[0], list_notes[:])
+        gather_scalar(notes_planes[:, 0, :], notes_pool[0], list_notes[:])
         gather_scalar(notes_planes[:, 1, :], notes_pool[1], list_notes[:])
-        gather_scalar(notes_planes[:, 2, :], notes_pool[2], list_notes[:])
+        gather_vector(notes_planes[:, 2, :], notes_pool[2], list_notes[:])
         notes_grouped = windows.tile([P, J, PACK], BF16, name="notes_grouped", align_bytes=64, offset=NOTES_GROUPED_AT)
         notes_codes, notes_scales = mx_tiles("notes", J)
         for h, (gather, copy) in enumerate(((gather_vector, nc.vector.tensor_copy), (gather_scalar, nc.scalar.copy))):

@@ -55,9 +55,9 @@ def tile_attend_tab_twosum_exchange_kernel(
             nc.sync.dma_start(tile[:].bitcast(I32), src[0].rearrange("p n t -> p (n t)").bitcast(I32))
             return tile
 
-        def zeroed_scale_tile(name, src):
+        def zeroed_scale_tile(name, src, engine):
             tile = keep.tile([P, src.shape[2]], U8, name=name)
-            nc.gpsimd.memset(tile[:].bitcast(I32), 0)
+            engine.memset(tile[:].bitcast(I32), 0)
             return tile
 
         def load_scale_rows(tile, src, row, c):
@@ -85,8 +85,8 @@ def tile_attend_tab_twosum_exchange_kernel(
         def interleave(copy, grouped, planes):
             copy(grouped.rearrange("p (c i) t -> p c t i", i=4), planes.rearrange("p t (c i) -> p c t i", i=4))
 
-        more_scale_pool = zeroed_scale_tile("more_scale_pool", more_scales)
-        keys_scale_pool = zeroed_scale_tile("keys_scale_pool", keys_scales)
+        more_scale_pool = zeroed_scale_tile("more_scale_pool", more_scales, nc.gpsimd)
+        keys_scale_pool = zeroed_scale_tile("keys_scale_pool", keys_scales, nc.vector)
         notes_rows = notes.rearrange("(p t) u -> t p u", t=PACK)
         users_rows = users2.rearrange("(p t) z -> t p z", t=PACK)
         more_pool = load_words("more_pool", more_words)
@@ -120,13 +120,13 @@ def tile_attend_tab_twosum_exchange_kernel(
             nc.sync.dma_start(window[:], vals[P * b : P * (b + 1), :])
             vals_pool.append(window)
 
-        identity_bf16 = keep.tile([P, P], BF16, name="identity_bf16")
+        identity_bf16 = keep.tile([P, P], BF16, name="identity_bf16", tag="users_planes")
         make_identity(nc, identity_bf16[:])
         identity = keep.tile([P, P], F32, name="identity")
         nc.scalar.activation(identity[:], identity_bf16[:], COPY)
 
         more_cd = gather_dealt("more_cd", U32, more_pool, list_more)
-        users_planes = keep.tile([P, PACK, J], BF16, name="users_planes")
+        users_planes = keep.tile([P, PACK, J], BF16, name="users_planes", tag="users_planes")
         for t in range(PACK):
             gather = gather_vector if t == 1 else gather_scalar
             gather(users_planes[:, t, :], users_pool[t], list_users[:])
@@ -139,13 +139,13 @@ def tile_attend_tab_twosum_exchange_kernel(
         notes_planes = keep.tile([P, PACK, J], BF16, name="notes_planes")
         gather_scalar(notes_planes[:, 0, :], notes_pool[0], list_notes[:])
         gather_scalar(notes_planes[:, 1, :], notes_pool[1], list_notes[:])
-        gather_vector(notes_planes[:, 2, :], notes_pool[2], list_notes[:])
         notes_grouped = windows.tile([P, J, PACK], BF16, name="notes_grouped", align_bytes=64, offset=NOTES_GROUPED_AT)
         notes_codes, notes_scales = mx_tiles("notes", J)
         for h, (gather, copy) in enumerate(((gather_vector, nc.vector.tensor_copy), (gather_scalar, nc.scalar.copy))):
             cols = slice(h * J // 2, (h + 1) * J // 2)
             entries = slice(h * LIST_COLS // 2, (h + 1) * LIST_COLS // 2)
-            gather(notes_planes[:, PACK - 1, cols], notes_pool[PACK - 1], list_notes[:, entries])
+            for t in range(2, PACK):
+                gather(notes_planes[:, t, cols], notes_pool[t], list_notes[:, entries])
             interleave(copy, notes_grouped[:, cols, :], notes_planes[:, :, cols])
             quantize(notes_codes[:, cols], notes_scales[:, cols], notes_grouped[:, cols, :].rearrange("p j t -> p (j t)"))
         keys_cd = windows.tile([P, I], U32, name="keys_cd", align_bytes=64, offset=NOTES_GROUPED_AT)

@@ -23,10 +23,9 @@ MORE_ROW = 4
 WINDOW_BYTES = 4 * T
 KEYS_AT = 4 * WINDOW_BYTES
 NOTES_GROUPED_AT = KEYS_AT + 4 * T
-VALS_GROUPED_AT = NOTES_GROUPED_AT + 2 * PACK * J
 BLOCK_BYTES = 2 * I
-PICKED_AT = (KEYS_AT, KEYS_AT + BLOCK_BYTES, WINDOW_BYTES, VALS_GROUPED_AT + BLOCK_BYTES // 2)
-GROUPED_AT = (WINDOW_BYTES, VALS_GROUPED_AT, VALS_GROUPED_AT + BLOCK_BYTES, VALS_GROUPED_AT + 2 * BLOCK_BYTES)
+PICKED_AT = (KEYS_AT, KEYS_AT + BLOCK_BYTES, KEYS_AT + BLOCK_BYTES, KEYS_AT + 3 * BLOCK_BYTES // 2)
+GROUPED_AT = (WINDOW_BYTES, KEYS_AT + 2 * BLOCK_BYTES)
 ACC_BANK = (("table0",), ("table1",), ("table2",), ("table3", "bank0"))
 
 
@@ -139,17 +138,21 @@ def tile_attend_tab_twosum_exchange_kernel(
         notes_planes = keep.tile([P, PACK, J], BF16, name="notes_planes")
         gather_scalar(notes_planes[:, 0, :], notes_pool[0], list_notes[:])
         gather_scalar(notes_planes[:, 1, :], notes_pool[1], list_notes[:])
-        notes_grouped = windows.tile([P, J, PACK], BF16, name="notes_grouped", align_bytes=64, offset=NOTES_GROUPED_AT)
+        notes_grouped = [
+            windows.tile([P, J // 2, PACK], BF16, name="notes_grouped0", align_bytes=64, offset=NOTES_GROUPED_AT),
+            keep.tile([P, J // 2, PACK], BF16, name="notes_grouped1", align_bytes=64),
+        ]
         notes_codes, notes_scales = mx_tiles("notes", J)
+        halves = [slice(h * J // 2, (h + 1) * J // 2) for h in range(2)]
         for h, (gather, copy) in enumerate(((gather_vector, nc.vector.tensor_copy), (gather_scalar, nc.scalar.copy))):
-            cols = slice(h * J // 2, (h + 1) * J // 2)
             entries = slice(h * LIST_COLS // 2, (h + 1) * LIST_COLS // 2)
             for t in range(2, PACK):
-                gather(notes_planes[:, t, cols], notes_pool[t], list_notes[:, entries])
-            interleave(copy, notes_grouped[:, cols, :], notes_planes[:, :, cols])
-            quantize(notes_codes[:, cols], notes_scales[:, cols], notes_grouped[:, cols, :].rearrange("p j t -> p (j t)"))
+                gather(notes_planes[:, t, halves[h]], notes_pool[t], list_notes[:, entries])
+            interleave(copy, notes_grouped[h][:], notes_planes[:, :, halves[h]])
+        quantize(notes_codes[:, halves[0]], notes_scales[:, halves[0]], notes_grouped[0][:].rearrange("p j t -> p (j t)"))
         keys_cd = windows.tile([P, I], U32, name="keys_cd", align_bytes=64, offset=NOTES_GROUPED_AT)
         nc.vector.tensor_copy(keys_cd[:].rearrange("q (r s) -> q s r", r=PACK), keys_pool[:].indirect(list_tokens[:]))
+        quantize(notes_codes[:, halves[1]], notes_scales[:, halves[1]], notes_grouped[1][:].rearrange("p j t -> p (j t)"))
 
         table = [psum.tile([P, PACK, P], F32, name="table%d" % c, tag="table%d" % c) for c in range(J // P)]
         terms = (
@@ -190,7 +193,7 @@ def tile_attend_tab_twosum_exchange_kernel(
 
         def pick(b):
             picked = windows.tile([P, I], BF16, name="picked%d" % b, offset=PICKED_AT[b])
-            if b < last - 1:
+            if b < last:
                 gather_scalar(picked[:], vals_pool[b], list_tokens[:])
             else:
                 gather_scalar(picked[:, : I // 2], vals_pool[b], list_tokens[:, : LIST_COLS // 2])
@@ -202,14 +205,19 @@ def tile_attend_tab_twosum_exchange_kernel(
             words = picked[:].bitcast(F32)
             for u in range(2):
                 nc.tensor.transpose(turned[:, u, :], words[:, u : I // 2 : 2], identity[:])
-            vals_grouped = windows.tile([P, P, PACK], BF16, name="vals_grouped%d" % b, align_bytes=64, offset=GROUPED_AT[b])
+            if b < len(GROUPED_AT):
+                vals_grouped = windows.tile([P, P, PACK], BF16, name="vals_grouped%d" % b, align_bytes=64, offset=GROUPED_AT[b])
+            else:
+                vals_grouped = keep.tile([P, P, PACK], BF16, name="vals_grouped%d" % b, align_bytes=64)
             nc.scalar.copy(vals_grouped[:].bitcast(F32), turned[:].rearrange("p u e -> p e u"))
             return vals_grouped
 
         def quantize_values(b, vals_grouped):
-            if b == 1:
-                vals_codes = windows.tile([P, P], U32, name="vals1_codes", align_bytes=64, offset=2 * WINDOW_BYTES + 4 * J)
-                vals_scales = keep.tile([P, P], U8, name="vals1_scales", align_bytes=64)
+            if b in (1, 2):
+                vals_codes = windows.tile(
+                    [P, P], U32, name="vals%d_codes" % b, align_bytes=64, offset=(b + 1) * WINDOW_BYTES + 8 * J
+                )
+                vals_scales = keep.tile([P, P], U8, name="vals%d_scales" % b, align_bytes=64)
             else:
                 vals_codes, vals_scales = mx_tiles("vals%d" % b, P, "weighted" if b == 0 else None)
             quantize(vals_codes[:], vals_scales[:], vals_grouped[:].rearrange("p e r -> p (e r)"))
@@ -239,15 +247,16 @@ def tile_attend_tab_twosum_exchange_kernel(
 
         picked_first = [pick(b) for b in range(2)]
         grouped_first = [turn(b, picked_first[b]) for b in range(2)]
-        operand0 = quantize_values(0, grouped_first[0])
+        result_first = keep.tile([P, J], F32, name="result_first")
+        multiply(0, quantize_values(0, grouped_first[0]), result_first)
         picked2 = pick(2)
-        result_first = windows.tile([P, J], F32, name="result_first", offset=2 * WINDOW_BYTES)
-        multiply(0, operand0, result_first)
         operand1 = quantize_values(1, grouped_first[1])
-        operand2 = quantize_values(2, turn(2, picked2))
+        grouped2 = turn(2, picked2)
         picked_last = pick(last)
+        operand2 = quantize_values(2, grouped2)
         result_middle = windows.tile([P, 2 * J], F32, name="result_middle", offset=last * WINDOW_BYTES)
         multiply(1, operand1, result_middle[:, :J])
+        grouped_last = turn(last, picked_last)
         multiply(2, operand2, result_middle[:, J:])
         result_last = keep.tile([P, J], F32, name="result_last")
-        multiply(last, quantize_values(last, turn(last, picked_last)), result_last)
+        multiply(last, quantize_values(last, grouped_last), result_last)

from contextlib import ExitStack

import concourse.mybir as mybir
from concourse.masks import make_identity

D, T, I, J, U, X, Z, E = 512, 2048, 512, 512, 1024, 1024, 1024, 512
FLOPS = 2 * (2 * D * I * J + I * E * J)

F32 = mybir.dt.float32
BF16 = mybir.dt.bfloat16
I32 = mybir.dt.int32
U32 = mybir.dt.uint32
U16 = mybir.dt.uint16
U8 = mybir.dt.uint8
FP8X4 = mybir.dt.float8_e4m3fn_x4
COPY = mybir.ActivationFunctionType.Copy
ALU = mybir.AluOpType

P = 128
PACK = 4
LIST_COLS = I // 16
MORE_ROW = 4
WINDOW_BYTES = 4 * T
KEYS_AT = 4 * WINDOW_BYTES
NOTES_GROUPED_AT = KEYS_AT + 4 * T
BLOCK_BYTES = 2 * I
PICKED_AT = (KEYS_AT, KEYS_AT + BLOCK_BYTES, KEYS_AT + BLOCK_BYTES, KEYS_AT + 3 * BLOCK_BYTES // 2)
GROUPED_AT = (WINDOW_BYTES, KEYS_AT + 2 * BLOCK_BYTES)
ACC_BANK = (("table0",), ("table1",), ("table2",), ("table3", "bank0"))


def tile_attend_tab_twosum_exchange_kernel(
    tc, keys_words, keys_scales, notes, more_words, more_scales, users2, rowf, vals, offs, offs2, offs3, offs4, out
):
    nc = tc.nc
    with ExitStack() as ctx:
        lists = ctx.enter_context(tc.tile_pool(name="lists", bufs=1))
        keep = ctx.enter_context(tc.tile_pool(name="keep", bufs=1))
        windows = ctx.enter_context(tc.tile_pool(name="windows", bufs=1))
        psum = ctx.enter_context(tc.psum_pool(name="psum", bufs=1))

        def load_list(name, src):
            tile = lists.tile([P, LIST_COLS], U16, name=name)
            nc.sync.dma_start(tile[:], src)
            return tile

        def load_rows(name, src):
            tile = keep.tile([P, src.shape[1]], F32, name=name, tag=name, align_bytes=64)
            nc.sync.dma_start(tile[:], src)
            return tile

        def load_words(name, src):
            tile = keep.tile([P, src.shape[2]], U32, name=name)
            nc.sync.dma_start(tile[:].bitcast(I32), src[0].rearrange("p n t -> p (n t)").bitcast(I32))
            return tile

        def zeroed_scale_tile(name, src, engine):
            tile = keep.tile([P, src.shape[2]], U8, name=name)
            engine.memset(tile[:].bitcast(I32), 0)
            return tile

        def load_scale_rows(tile, src, row, c):
            nc.sync.dma_start(tile[row + c : P : 32, :].bitcast(I32), src[0, c:16:4, :].bitcast(I32))

        def gather_scalar(dst, window, offsets):
            nc.scalar.activation(dst, window[:].indirect(offsets), COPY)

        def gather_vector(dst, window, offsets):
            nc.vector.tensor_copy(dst, window[:].indirect(offsets))

        def gather_dealt(name, dtype, window, offsets):
            tile = keep.tile([P, I], dtype, name=name, align_bytes=64)
            nc.vector.tensor_copy(tile[:].rearrange("q (r s) -> q s r", r=PACK), window[:].indirect(offsets[:]))
            return tile

        def mx_tiles(name, width, codes_tag=None):
            codes = keep.tile([P, width], U32, name=name + "_codes", tag=codes_tag or name + "_codes", align_bytes=64)
            scales = keep.tile([P, width], U8, name=name + "_scales", align_bytes=64)
            return codes, scales

        def quantize(codes, scales, grouped):
            nc.vector.quantize_mx(out=codes.bitcast(FP8X4), scales=scales, in_=grouped)

        def interleave(copy, grouped, planes):
            copy(grouped.rearrange("p (c i) t -> p c t i", i=4), planes.rearrange("p t (c i) -> p c t i", i=4))

        more_scale_pool = zeroed_scale_tile("more_scale_pool", more_scales, nc.gpsimd)
        keys_scale_pool = zeroed_scale_tile("keys_scale_pool", keys_scales, nc.vector)
        notes_rows = notes.rearrange("(p t) u -> t p u", t=PACK)
        users_rows = users2.rearrange("(p t) z -> t p z", t=PACK)
        more_pool = load_words("more_pool", more_words)
        list_more = load_list("list_more", offs3)
        users_pool = [load_rows("users0", users_rows[0])]
        list_users = load_list("list_users", offs4)
        load_scale_rows(more_scale_pool, more_scales, MORE_ROW, 0)
        load_scale_rows(more_scale_pool, more_scales, MORE_ROW, 1)
        users_pool.append(load_rows("users1", users_rows[1]))
        load_scale_rows(more_scale_pool, more_scales, MORE_ROW, 2)
        load_scale_rows(more_scale_pool, more_scales, MORE_ROW, 3)
        users_pool.append(load_rows("users2", users_rows[2]))
        list_tokens = load_list("list_tokens", offs)
        load_scale_rows(keys_scale_pool, keys_scales, 0, 0)
        users_pool.append(load_rows("users3", users_rows[3]))
        load_scale_rows(keys_scale_pool, keys_scales, 0, 1)
        load_scale_rows(keys_scale_pool, keys_scales, 0, 2)
        load_scale_rows(keys_scale_pool, keys_scales, 0, 3)
        notes_pool = [load_rows("notes0", notes_rows[0])]
        list_notes = load_list("list_notes", offs2)
        notes_pool.append(load_rows("notes1", notes_rows[1]))
        factor = keep.tile([P, PACK], F32, name="factor")
        nc.sync.dma_start(factor[:], rowf.rearrange("(p r) o -> p (r o)", r=PACK))
        notes_pool.append(load_rows("notes2", notes_rows[2]))
        notes_pool.append(load_rows("notes3", notes_rows[3]))
        keys_pool = windows.tile([P, T], U32, name="keys_pool", offset=KEYS_AT)
        nc.sync.dma_start(keys_pool[:].bitcast(I32), keys_words[0].rearrange("p n t -> p (n t)").bitcast(I32))
        vals_pool = []
        for b in range(E // P):
            window = windows.tile([P, T], F32, name="vals%d" % b, offset=b * WINDOW_BYTES)
            nc.sync.dma_start(window[:], vals[P * b : P * (b + 1), :])
            vals_pool.append(window)

        identity_bf16 = keep.tile([P, P], BF16, name="identity_bf16", tag="users_planes")
        make_identity(nc, identity_bf16[:])
        identity = keep.tile([P, P], F32, name="identity")
        nc.scalar.activation(identity[:], identity_bf16[:], COPY)

        more_cd = gather_dealt("more_cd", U32, more_pool, list_more)
        users_planes = keep.tile([P, PACK, J], BF16, name="users_planes", tag="users_planes")
        for t in range(PACK):
            gather = gather_vector if t == 1 else gather_scalar
            gather(users_planes[:, t, :], users_pool[t], list_users[:])
        more_sc = gather_dealt("more_sc", U8, more_scale_pool, list_more)
        keys_sc = gather_dealt("keys_sc", U8, keys_scale_pool, list_tokens)
        users_grouped = keep.tile([P, J, PACK], BF16, name="users_grouped", align_bytes=64)
        interleave(nc.vector.tensor_copy, users_grouped[:], users_planes[:])
        users_codes, users_scales = mx_tiles("users", J)
        quantize(users_codes[:], users_scales[:], users_grouped[:].rearrange("p j t -> p (j t)"))
        notes_planes = keep.tile([P, PACK, J], BF16, name="notes_planes")
        gather_scalar(notes_planes[:, 0, :], notes_pool[0], list_notes[:])
        gather_scalar(notes_planes[:, 1, :], notes_pool[1], list_notes[:])
        notes_grouped = [
            windows.tile([P, J // 2, PACK], BF16, name="notes_grouped0", align_bytes=64, offset=NOTES_GROUPED_AT),
            keep.tile([P, J // 2, PACK], BF16, name="notes_grouped1", align_bytes=64),
        ]
        notes_codes, notes_scales = mx_tiles("notes", J)
        halves = [slice(h * J // 2, (h + 1) * J // 2) for h in range(2)]
        for h, (gather, copy) in enumerate(((gather_vector, nc.vector.tensor_copy), (gather_scalar, nc.scalar.copy))):
            entries = slice(h * LIST_COLS // 2, (h + 1) * LIST_COLS // 2)
            for t in range(2, PACK):
                gather(notes_planes[:, t, halves[h]], notes_pool[t], list_notes[:, entries])
            interleave(copy, notes_grouped[h][:], notes_planes[:, :, halves[h]])
        quantize(notes_codes[:, halves[0]], notes_scales[:, halves[0]], notes_grouped[0][:].rearrange("p j t -> p (j t)"))
        keys_cd = windows.tile([P, I], U32, name="keys_cd", align_bytes=64, offset=NOTES_GROUPED_AT)
        nc.vector.tensor_copy(keys_cd[:].rearrange("q (r s) -> q s r", r=PACK), keys_pool[:].indirect(list_tokens[:]))
        quantize(notes_codes[:, halves[1]], notes_scales[:, halves[1]], notes_grouped[1][:].rearrange("p j t -> p (j t)"))

        table = [psum.tile([P, PACK, P], F32, name="table%d" % c, tag="table%d" % c) for c in range(J // P)]
        terms = (
            (more_cd, more_sc, MORE_ROW, users_codes, users_scales),
            (keys_cd, keys_sc, 0, notes_codes, notes_scales),
        )
        for term, (lhs_codes, lhs_scales, row, rhs_codes, rhs_scales) in enumerate(terms):
            for c in range(J // P):
                cols = slice(P * c, P * (c + 1))
                for r in range(PACK):
                    rows = slice(P * r, P * (r + 1))
                    nc.tensor.matmul_mx(
                        out=table[c][:, r, :],
                        lhsT=lhs_codes[:, rows].bitcast(FP8X4),
                        lhsT_scale=lhs_scales[row:P, rows],
                        rhs=rhs_codes[:, cols].bitcast(FP8X4),
                        rhs_scale=rhs_scales[:, cols],
                        start=(term == 0 and r == 0),
                        stop=(term == len(terms) - 1 and r == PACK - 1),
                    )

        weighted = keep.tile([P, J, PACK], BF16, name="weighted", tag="weighted", align_bytes=64)
        weighted_codes, weighted_scales = mx_tiles("weighted", J)
        for c in range(J // P):
            nc.vector.scalar_tensor_tensor(
                out=weighted[:, P * c : P * (c + 1), :],
                in0=table[c][:].rearrange("p r j -> p j r"),
                scalar=0.0,
                in1=factor[:].unsqueeze(1).to_broadcast([P, P, PACK]),
                op0=ALU.max,
                op1=ALU.mult,
            )
        for h in range(2):
            cols = slice(h * J // 2, (h + 1) * J // 2)
            quantize(weighted_codes[:, cols], weighted_scales[:, cols], weighted[:, cols, :].rearrange("p j r -> p (j r)"))

        last = E // P - 1

        def pick(b):
            picked = windows.tile([P, I], BF16, name="picked%d" % b, offset=PICKED_AT[b])
            if b < last:
                gather_scalar(picked[:], vals_pool[b], list_tokens[:])
            else:
                gather_scalar(picked[:, : I // 2], vals_pool[b], list_tokens[:, : LIST_COLS // 2])
                gather_vector(picked[:, I // 2 :], vals_pool[b], list_tokens[:, LIST_COLS // 2 :])
            return picked

        def turn(b, picked):
            turned = psum.tile([P, 2, P], F32, name="turned%d" % b, tag="bank%d" % b)
            words = picked[:].bitcast(F32)
            for u in range(2):
                nc.tensor.transpose(turned[:, u, :], words[:, u : I // 2 : 2], identity[:])
            if b < len(GROUPED_AT):
                vals_grouped = windows.tile([P, P, PACK], BF16, name="vals_grouped%d" % b, align_bytes=64, offset=GROUPED_AT[b])
            else:
                vals_grouped = keep.tile([P, P, PACK], BF16, name="vals_grouped%d" % b, align_bytes=64)
            nc.scalar.copy(vals_grouped[:].bitcast(F32), turned[:].rearrange("p u e -> p e u"))
            return vals_grouped

        def quantize_values(b, vals_grouped):
            if b in (1, 2):
                vals_codes = windows.tile(
                    [P, P], U32, name="vals%d_codes" % b, align_bytes=64, offset=(b + 1) * WINDOW_BYTES + 8 * J
                )
                vals_scales = keep.tile([P, P], U8, name="vals%d_scales" % b, align_bytes=64)
            else:
                vals_codes, vals_scales = mx_tiles("vals%d" % b, P, "weighted" if b == 0 else None)
            quantize(vals_codes[:], vals_scales[:], vals_grouped[:].rearrange("p e r -> p (e r)"))
            return vals_codes, vals_scales

        def multiply(b, operand, result):
            vals_codes, vals_scales = operand
            parts = 1 if b < last else 2
            for h in range(parts):
                cols = slice(h * J // parts, (h + 1) * J // parts)
                acc = psum.tile([P, J // parts], F32, name="acc%d_%d" % (b, h), tag=ACC_BANK[b][h])
                nc.tensor.matmul_mx(
                    out=acc[:],
                    lhsT=vals_codes[:].bitcast(FP8X4),
                    lhsT_scale=vals_scales[:],
                    rhs=weighted_codes[:, cols].bitcast(FP8X4),
                    rhs_scale=weighted_scales[:, cols],
                    start=True,
                    stop=True,
                )
                if b >= last - 1 and h == 0:
                    nc.scalar.copy(result[:, cols], acc[:])
                else:
                    nc.vector.tensor_copy(result[:, cols], acc[:])
                queue = nc.scalar if b == last and h == 0 else nc.sync
                queue.dma_start(out[P * b : P * (b + 1), cols], result[:, cols])

        picked_first = [pick(b) for b in range(2)]
        grouped_first = [turn(b, picked_first[b]) for b in range(2)]
        result_first = keep.tile([P, J], F32, name="result_first")
        multiply(0, quantize_values(0, grouped_first[0]), result_first)
        picked2 = pick(2)
        operand1 = quantize_values(1, grouped_first[1])
        grouped2 = turn(2, picked2)
        picked_last = pick(last)
        operand2 = quantize_values(2, grouped2)
        result_middle = windows.tile([P, 2 * J], F32, name="result_middle", offset=last * WINDOW_BYTES)
        multiply(1, operand1, result_middle[:, :J])
        grouped_last = turn(last, picked_last)
        multiply(2, operand2, result_middle[:, J:])
        result_last = keep.tile([P, J], F32, name="result_last")
        multiply(last, quantize_values(last, grouped_last), result_last)
